import numpy as np
import ml_dtypes


def mxq(x, axis, fmt="e4m3"):
    dtype, down = {"e4m3": (ml_dtypes.float8_e4m3fn, 7), "e5m2": (ml_dtypes.float8_e5m2, 14)}[fmt]
    v = np.moveaxis(np.asarray(x, np.float32).astype(ml_dtypes.bfloat16).astype(np.float64), axis, -1)
    blocks = v.reshape(v.shape[:-1] + (-1, 32))
    amax = np.abs(blocks).max(-1, keepdims=True)
    byte = np.maximum(np.where(amax > 0, np.frexp(amax)[1] - 1 + 127, 0) - down, 1)
    scale = np.exp2(byte - 127.0)
    codes = (blocks / scale).astype(np.float32).astype(dtype).astype(np.float64)
    return np.moveaxis((codes * scale).reshape(v.shape), -1, axis)


WIDE = False


def mx_kscale(k):
    if not WIDE:
        return np.ones(k)
    levels = np.array([10, -10, 5, -5, 0])
    if k % 512:
        return np.exp2(np.random.permutation(np.resize(levels, k // 32))).repeat(32)
    a = np.empty((k // 512, 16))
    for p in range(k // 512):
        a[p, :8] = np.random.permutation(np.resize(levels, 8))
        for g in range(8):
            far = levels[np.abs(levels - a[p, g]) >= 10]
            a[p, g + 8] = far[np.random.randint(len(far))]
    return np.exp2(a.ravel()).repeat(32)


def f64(x):
    return np.asarray(x).astype(np.float64)


def striped(idx):
    return np.tile(idx.reshape(-1, 16).T, (8, 1)).astype(np.uint16)


def unstriped(offs):
    return offs[:16].T.reshape(-1).astype(np.int64)


def striped8(idx):
    return np.concatenate([x.reshape(-1, 16).T for x in idx]).astype(np.uint16)


def runs(offs, k):
    lists = np.stack([offs[16 * r : 16 * r + 16].T.reshape(-1) for r in range(8)]).astype(np.int64)
    return lists[np.arange(k) % 512 // 64]


def pack_weight(w):
    k, n = w.shape
    w = f64(np.asarray(w, np.float32).astype(ml_dtypes.bfloat16)).reshape(k // 32, 32, n)
    amax = np.abs(w).max(1)
    byte = np.clip(np.where(amax > 0, np.frexp(amax)[1] - 1 + 127 - 7, 1), 1, 254)
    scaled = (w * np.exp2(127.0 - byte)[:, None, :]).reshape(k, n).astype(np.float32)
    words = np.ascontiguousarray(scaled.reshape(k // 512, 128, 4, n).transpose(0, 1, 3, 2)).astype(ml_dtypes.float8_e4m3fn).view(np.uint8)
    return words, np.ascontiguousarray(byte.astype(np.uint8).reshape(k // 512, 16, n))


def unpack_weight(words, scales):
    g, p, n, _ = words.shape
    vals = np.ascontiguousarray(words).view(ml_dtypes.float8_e4m3fn).astype(np.float64) * np.repeat(np.exp2(scales.astype(np.float64) - 127.0), 8, axis=1)[..., None]
    return vals.transpose(0, 1, 3, 2).reshape(g * 512, n)


K, T, S, H, C = 512, 2048, 512, 512, 512


def setup_inputs():
    n = np.random.standard_normal
    s = mx_kscale(K)[:, None]
    packed_xT = pack_weight(n((K, T)) * s)
    return {
        "x_words": packed_xT[0],
        "x_scales": packed_xT[1],
        "w1": (n((K, H)) / np.sqrt(K) / s).astype(np.float32),
        "gs": (np.random.uniform(0.5, 1.5, (K, 1)) / s).astype(np.float32),
        "wb": (n((K, S)) / np.sqrt(K) / s).astype(np.float32),
        "offs": striped(np.random.permutation(T)[:S]),
        "n1": striped(np.random.permutation(S)),
        "n2": striped(np.random.permutation(S)),
        "cand": striped(np.random.permutation(T)[:C]),
        "cb": striped(np.random.permutation(T)[:C]),
        "n3": striped8(np.stack([np.random.permutation(S) for _ in range(8)])),
        "n4": striped8(np.stack([np.random.permutation(S) for _ in range(8)])),
        "n5": striped8(np.stack([np.random.permutation(S) for _ in range(8)])),
        "n6": striped8(np.stack([np.random.permutation(S) for _ in range(8)])),
    }


def reference(x_words, x_scales, w1, gs, wb, offs, n1, n2, cand, cb, n3, n4, n5, n6):
    x_cand = unpack_weight(x_words, x_scales)[:, unstriped(cand)]
    xq = unpack_weight(x_words, x_scales)[:, unstriped(offs)]
    y = mxq(f64(w1), 0, "e4m3").T @ xq
    pa = y[:, unstriped(n1)]
    pb = y[:, unstriped(n2)]
    z = f64(gs) * (np.maximum(np.minimum(y, pa), np.minimum(np.maximum(y, pa), pb)))
    a = 0.0625 * ((x_cand.T @ mxq(z, 0, "e4m3")))
    x_cb = unpack_weight(x_words, x_scales)[:, unstriped(cb)]
    b = x_cb.T @ mxq(f64(wb), 0, "e4m3")
    return np.maximum(a[np.arange(C)[:, None], runs(n3, C)] + b[np.arange(C)[:, None], runs(n5, C)], a[np.arange(C)[:, None], runs(n4, C)] + b[np.arange(C)[:, None], runs(n6, C)])

@@ -1,0 +1,214 @@
+from contextlib import ExitStack
+
+import concourse.mybir as mybir
+
+K, T, S, H, C = 512, 2048, 512, 512, 512
+FLOPS = 2 * K * (H * S + C * S + C * S)
+
+F32 = mybir.dt.float32
+BF16 = mybir.dt.bfloat16
+I32 = mybir.dt.int32
+U32 = mybir.dt.uint32
+U16 = mybir.dt.uint16
+U8 = mybir.dt.uint8
+FP8X4 = mybir.dt.float8_e4m3fn_x4
+ALU = mybir.AluOpType
+COPY = mybir.ActivationFunctionType.Copy
+
+P = 128
+PACK = 4
+TILES = 4
+WINDOW = 2 * S
+
+
+def tile_picked_cdswpathbmed_none_p_kernel(
+    tc, x_words, x_scales, w1, gs, wb, offs, n1, n2, cand, cb, n3, n4, n5, n6, out
+):
+    nc = tc.nc
+    with ExitStack() as ctx:
+        lists = ctx.enter_context(tc.tile_pool(name="lists", bufs=1))
+        keep = ctx.enter_context(tc.tile_pool(name="keep", bufs=1))
+        psum = ctx.enter_context(tc.psum_pool(name="psum", bufs=1))
+
+        def load_list(name, source):
+            tile = lists.tile([P, S // 16], U16, name=name)
+            nc.sync.dma_start(tile[:], source)
+            return tile
+
+        x_s = keep.tile([P, T], U8, name="x_s", align_bytes=64)
+        nc.vector.memset(x_s[:].bitcast(I32), 0)
+
+        w1_rows = w1.rearrange("(p j) h -> p j h", j=PACK)
+        w1_raw = [keep.tile([P, PACK, H // 2], F32, name=f"w1_raw{u}", tag=f"raw{u}") for u in range(2)]
+        l_offs = load_list("l_offs", offs)
+        nc.sync.dma_start(w1_raw[0][:], w1_rows[:, :, : H // 2])
+        for q in range(4):
+            nc.sync.dma_start(
+                x_s[32 * q : 32 * q + 4, :].bitcast(I32),
+                x_scales[0, 4 * q : 4 * q + 4, :].bitcast(I32),
+            )
+        l_cand = load_list("l_cand", cand)
+        nc.sync.dma_start(w1_raw[1][:], w1_rows[:, :, H // 2 :])
+        x_w = keep.tile([P, T], I32, name="x_w", align_bytes=64)
+        nc.sync.dma_start(x_w[:], x_words[0].rearrange("p n t -> p (n t)").bitcast(I32))
+        l_cb = load_list("l_cb", cb)
+        gain = keep.tile([P, TILES], F32, name="gain")
+        nc.sync.dma_start(gain[:], gs.rearrange("(p t) o -> p (t o)", t=TILES))
+        l_n1 = load_list("l_n1", n1)
+        l_n2 = load_list("l_n2", n2)
+        l_n5 = load_list("l_n5", n5)
+        l_n6 = load_list("l_n6", n6)
+        l_n3 = load_list("l_n3", n3)
+        l_n4 = load_list("l_n4", n4)
+
+        def gather_scales(name, entries):
+            picked = keep.tile([P, S], U8, name=name, align_bytes=64)
+            nc.vector.tensor_copy(picked[:], x_s[:].indirect(entries[:]))
+            return picked
+
+        def deal_scales(name, picked):
+            dealt = keep.tile([P, S], U8, name=name, align_bytes=64)
+            nc.vector.tensor_copy(
+                dealt[:].bitcast(I32).rearrange("p (t q) -> p t q", t=TILES),
+                picked[:].bitcast(I32).rearrange("p (q t) -> p t q", t=TILES),
+            )
+            return dealt
+
+        def gather_words_dealt(name, entries):
+            dealt = keep.tile([P, S], U32, name=name, align_bytes=64)
+            nc.vector.tensor_copy(
+                dealt[:].rearrange("p (t q b) -> p q t b", t=TILES, b=4),
+                x_w[:].bitcast(U32).indirect(entries[:]),
+            )
+            return dealt
+
+        offs_s = gather_scales("offs_s", l_offs)
+        cand_s = deal_scales("cand_s", gather_scales("cand_s_picked", l_cand))
+
+        w1_b = keep.tile([P, H * PACK], BF16, name="w1_b", align_bytes=64)
+        w1_dealt = w1_b[:].rearrange("p (t m j) -> p m j t", t=TILES, j=PACK)
+        for u in range(2):
+            nc.scalar.activation(
+                w1_dealt[:, u * (P // 2) : (u + 1) * (P // 2)],
+                w1_raw[u][:].rearrange("p j (m t) -> p m j t", t=TILES),
+                COPY,
+            )
+        wb_rows = wb.rearrange("(p j) n -> p j n", j=PACK)
+        wb_raw = []
+        for u in range(2):
+            tile = keep.tile([P, PACK, S // 2], F32, name=f"wb_raw{u}", tag=f"raw{u}")
+            nc.sync.dma_start(tile[:], wb_rows[:, :, u * (S // 2) : (u + 1) * (S // 2)])
+            wb_raw.append(tile)
+
+        offs_w = keep.tile([P, S], U32, name="offs_w", align_bytes=64)
+        nc.vector.tensor_copy(offs_w[:], x_w[:].bitcast(U32).indirect(l_offs[:]))
+
+        w1_w = keep.tile([P, H], U32, name="w1_w", align_bytes=64)
+        w1_s = keep.tile([P, H], U8, name="w1_s", align_bytes=64)
+        y_ps = []
+        for t in range(TILES):
+            cols = slice(t * P, (t + 1) * P)
+            nc.vector.quantize_mx(
+                w1_w[:, cols].bitcast(FP8X4), w1_s[:, cols], w1_b[:, t * P * PACK : (t + 1) * P * PACK]
+            )
+            bank = psum.tile([P, S], F32, name=f"y_ps{t}", tag=f"bank{t}")
+            nc.tensor.matmul_mx(
+                bank[:], lhsT=w1_w[:, cols].bitcast(FP8X4), lhsT_scale=w1_s[:, cols],
+                rhs=offs_w[:].bitcast(FP8X4), rhs_scale=offs_s[:], start=True, stop=True,
+            )
+            y_ps.append(bank)
+
+        cand_w = gather_words_dealt("cand_w", l_cand)
+        cb_s = deal_scales("cb_s", gather_scales("cb_s_picked", l_cb))
+        cb_w = gather_words_dealt("cb_w", l_cb)
+
+        wb_b = keep.tile([P, S * PACK], BF16, name="wb_b", align_bytes=64)
+        for u in range(2):
+            nc.vector.tensor_copy(
+                wb_b[:, u * S * 2 : (u + 1) * S * 2].rearrange("p (c i j) -> p c j i", i=4, j=PACK),
+                wb_raw[u][:].rearrange("p j (c i) -> p c j i", i=4),
+            )
+        wb_w = keep.tile([P, S], U32, name="wb_w", align_bytes=64)
+        wb_s = keep.tile([P, S], U8, name="wb_s", align_bytes=64)
+        nc.vector.quantize_mx(wb_w[:].bitcast(FP8X4), wb_s[:], wb_b[:])
+
+        low = keep.tile([P, TILES, S], F32, name="low")
+        upper = keep.tile([P, TILES, S], F32, name="upper")
+        for t in range(TILES):
+            y = keep.tile([P, WINDOW], F32, name=f"y{t}")
+            nc.scalar.activation(y[:, :S], y_ps[t][:], COPY, scale=gain[:, t : t + 1])
+            pa = keep.tile([P, S], F32, name=f"pa{t}")
+            pb = keep.tile([P, S], F32, name=f"pb{t}")
+            high = keep.tile([P, S], F32, name=f"high{t}")
+            nc.scalar.activation(pa[:], y[:].indirect(l_n1[:]), COPY)
+            nc.scalar.activation(pb[:], y[:].indirect(l_n2[:]), COPY)
+            nc.vector.tensor_tensor(low[:, t, :], y[:, :S], pa[:], ALU.min)
+            nc.vector.tensor_tensor(high[:], y[:, :S], pa[:], ALU.max)
+            nc.vector.tensor_tensor(upper[:, t, :], high[:], pb[:], ALU.min)
+
+        z_b = keep.tile([P, S * PACK], BF16, name="z_b", align_bytes=64)
+        z_w = keep.tile([P, S], U32, name="z_w", align_bytes=64)
+        z_s = keep.tile([P, S], U8, name="z_s", align_bytes=64)
+        half = S // 2
+        for u in range(2):
+            cols = slice(u * half, (u + 1) * half)
+            nc.vector.tensor_tensor(
+                z_b[:, u * half * PACK : (u + 1) * half * PACK].rearrange("p (c i t) -> p c t i", i=4, t=TILES),
+                low[:, :, cols].rearrange("p t (c i) -> p c t i", i=4),
+                upper[:, :, cols].rearrange("p t (c i) -> p c t i", i=4),
+                ALU.max,
+            )
+        for u in range(2):
+            cols = slice(u * half, (u + 1) * half)
+            nc.vector.quantize_mx(
+                z_w[:, cols].bitcast(FP8X4), z_s[:, cols], z_b[:, u * half * PACK : (u + 1) * half * PACK]
+            )
+
+        b_rows = []
+        for t in range(TILES):
+            cols = slice(t * P, (t + 1) * P)
+            bank = psum.tile([P, S], F32, name=f"b_ps{t}", tag=f"bank{TILES + t}")
+            nc.tensor.matmul_mx(
+                bank[:], lhsT=cb_w[:, cols].bitcast(FP8X4), lhsT_scale=cb_s[:, cols],
+                rhs=wb_w[:].bitcast(FP8X4), rhs_scale=wb_s[:], start=True, stop=True,
+            )
+            b = keep.tile([P, WINDOW], F32, name=f"b{t}")
+            nc.scalar.activation(b[:, :S], bank[:], COPY)
+            b_rows.append(b)
+
+        out_rows = out.rearrange("(q t b) j -> t q b j", t=TILES, b=4)
+        for t in range(TILES):
+            cols = slice(t * P, (t + 1) * P)
+            a = keep.tile([P, WINDOW], F32, name=f"a{t}")
+            if t == 0:
+                for u in range(2):
+                    part = slice(u * half, (u + 1) * half)
+                    bank = psum.tile([P, half], F32, name=f"a_ps0_{u}", tag=f"bank{TILES * u}")
+                    nc.tensor.matmul_mx(
+                        bank[:], lhsT=cand_w[:, cols].bitcast(FP8X4), lhsT_scale=cand_s[:, cols],
+                        rhs=z_w[:, part].bitcast(FP8X4), rhs_scale=z_s[:, part], start=True, stop=True,
+                    )
+                    nc.vector.tensor_scalar(a[:, part], bank[:], 0.0625, None, ALU.mult)
+            else:
+                bank = psum.tile([P, S], F32, name=f"a_ps{t}", tag=f"bank{t}")
+                nc.tensor.matmul_mx(
+                    bank[:], lhsT=cand_w[:, cols].bitcast(FP8X4), lhsT_scale=cand_s[:, cols],
+                    rhs=z_w[:].bitcast(FP8X4), rhs_scale=z_s[:], start=True, stop=True,
+                )
+                nc.scalar.activation(a[:, :S], bank[:], COPY, scale=0.0625)
+            b5 = keep.tile([P, S], F32, name=f"b5_{t}", tag="b5", bufs=2)
+            b6 = keep.tile([P, S], F32, name=f"b6_{t}", tag="b6", bufs=2)
+            nc.scalar.activation(b5[:], b_rows[t][:].indirect(l_n5[:]), COPY)
+            nc.scalar.activation(b6[:], b_rows[t][:].indirect(l_n6[:]), COPY)
+            s1 = keep.tile([P, S], F32, name=f"s1_{t}")
+            s2 = keep.tile([P, S], F32, name=f"s2_{t}")
+            nc.vector.tensor_tensor(s1[:], a[:].indirect(l_n3[:]), b5[:], ALU.add)
+            if t == TILES - 1:
+                a4 = keep.tile([P, S], F32, name="a4")
+                nc.scalar.activation(a4[:], a[:].indirect(l_n4[:]), COPY)
+                nc.vector.tensor_tensor(s2[:], a4[:], b6[:], ALU.add)
+            else:
+                nc.vector.tensor_tensor(s2[:], a[:].indirect(l_n4[:]), b6[:], ALU.add)
+            best = keep.tile([P, S], F32, name=f"best{t}")
+            nc.vector.tensor_tensor(best[:], s1[:], s2[:], ALU.max)
+            nc.sync.dma_start(out_rows[t], best[:])

@@ -19,6 +19,11 @@ P = 128
 PACK = 4
 TILES = 4
 WINDOW = 2 * S
+HALF = S // 2
+FIRST = 2
+BUFS = 3
+EARLY = 256
+SPLIT = 2
 
 
 def tile_picked_cdswpathbmed_none_p_kernel(
@@ -38,17 +43,21 @@ def tile_picked_cdswpathbmed_none_p_kernel(
         x_s = keep.tile([P, T], U8, name="x_s", align_bytes=64)
         nc.vector.memset(x_s[:].bitcast(I32), 0)
 
-        w1_rows = w1.rearrange("(p j) h -> p j h", j=PACK)
-        w1_raw = [keep.tile([P, PACK, H // 2], F32, name=f"w1_raw{u}", tag=f"raw{u}") for u in range(2)]
+        def load_half(name, weights, u):
+            rows = weights.rearrange("(p j) n -> p j n", j=PACK)
+            tile = keep.tile([P, PACK, HALF], F32, name=f"{name}{u}")
+            nc.sync.dma_start(tile[:], rows[:, :, u * HALF : (u + 1) * HALF])
+            return tile
+
+        l_cand = load_list("l_cand", cand)
+        w1_raw = [load_half("w1_raw", w1, 0)]
         l_offs = load_list("l_offs", offs)
-        nc.sync.dma_start(w1_raw[0][:], w1_rows[:, :, : H // 2])
         for q in range(4):
             nc.sync.dma_start(
                 x_s[32 * q : 32 * q + 4, :].bitcast(I32),
                 x_scales[0, 4 * q : 4 * q + 4, :].bitcast(I32),
             )
-        l_cand = load_list("l_cand", cand)
-        nc.sync.dma_start(w1_raw[1][:], w1_rows[:, :, H // 2 :])
+        w1_raw.append(load_half("w1_raw", w1, 1))
         x_w = keep.tile([P, T], I32, name="x_w", align_bytes=64)
         nc.sync.dma_start(x_w[:], x_words[0].rearrange("p n t -> p (n t)").bitcast(I32))
         l_cb = load_list("l_cb", cb)
@@ -56,14 +65,18 @@ def tile_picked_cdswpathbmed_none_p_kernel(
         nc.sync.dma_start(gain[:], gs.rearrange("(p t) o -> p (t o)", t=TILES))
         l_n1 = load_list("l_n1", n1)
         l_n2 = load_list("l_n2", n2)
+        wb_raw = [load_half("wb_raw", wb, u) for u in range(2)]
         l_n5 = load_list("l_n5", n5)
         l_n6 = load_list("l_n6", n6)
         l_n3 = load_list("l_n3", n3)
         l_n4 = load_list("l_n4", n4)
 
-        def gather_scales(name, entries):
+        def entries(tile, part):
+            return tile[:, part.start // 16 : part.stop // 16]
+
+        def gather_scales(name, picks):
             picked = keep.tile([P, S], U8, name=name, align_bytes=64)
-            nc.vector.tensor_copy(picked[:], x_s[:].indirect(entries[:]))
+            nc.vector.tensor_copy(picked[:], x_s[:].indirect(picks[:]))
             return picked
 
         def deal_scales(name, picked):
@@ -74,16 +87,18 @@ def tile_picked_cdswpathbmed_none_p_kernel(
             )
             return dealt
 
-        def gather_words_dealt(name, entries):
+        def gather_words_dealt(name, picks):
             dealt = keep.tile([P, S], U32, name=name, align_bytes=64)
             nc.vector.tensor_copy(
                 dealt[:].rearrange("p (t q b) -> p q t b", t=TILES, b=4),
-                x_w[:].bitcast(U32).indirect(entries[:]),
+                x_w[:].bitcast(U32).indirect(picks[:]),
             )
             return dealt
 
+        halves = [slice(u * HALF, (u + 1) * HALF) for u in range(2)]
+
+        cand_s_picked = gather_scales("cand_s_picked", l_cand)
         offs_s = gather_scales("offs_s", l_offs)
-        cand_s = deal_scales("cand_s", gather_scales("cand_s_picked", l_cand))
 
         w1_b = keep.tile([P, H * PACK], BF16, name="w1_b", align_bytes=64)
         w1_dealt = w1_b[:].rearrange("p (t m j) -> p m j t", t=TILES, j=PACK)
@@ -93,122 +108,143 @@ def tile_picked_cdswpathbmed_none_p_kernel(
                 w1_raw[u][:].rearrange("p j (m t) -> p m j t", t=TILES),
                 COPY,
             )
-        wb_rows = wb.rearrange("(p j) n -> p j n", j=PACK)
-        wb_raw = []
-        for u in range(2):
-            tile = keep.tile([P, PACK, S // 2], F32, name=f"wb_raw{u}", tag=f"raw{u}")
-            nc.sync.dma_start(tile[:], wb_rows[:, :, u * (S // 2) : (u + 1) * (S // 2)])
-            wb_raw.append(tile)
-
-        offs_w = keep.tile([P, S], U32, name="offs_w", align_bytes=64)
-        nc.vector.tensor_copy(offs_w[:], x_w[:].bitcast(U32).indirect(l_offs[:]))
-
         w1_w = keep.tile([P, H], U32, name="w1_w", align_bytes=64)
         w1_s = keep.tile([P, H], U8, name="w1_s", align_bytes=64)
-        y_ps = []
-        for t in range(TILES):
+        nc.vector.quantize_mx(w1_w[:].bitcast(FP8X4), w1_s[:], w1_b[:])
+
+        offs_w = keep.tile([P, S], U32, name="offs_w", align_bytes=64)
+        for part in halves:
+            nc.vector.tensor_copy(offs_w[:, part], x_w[:].bitcast(U32).indirect(entries(l_offs, part)))
+
+        def product(bank, t, left_w, left_s, right_w, right_s):
             cols = slice(t * P, (t + 1) * P)
-            nc.vector.quantize_mx(
-                w1_w[:, cols].bitcast(FP8X4), w1_s[:, cols], w1_b[:, t * P * PACK : (t + 1) * P * PACK]
-            )
-            bank = psum.tile([P, S], F32, name=f"y_ps{t}", tag=f"bank{t}")
             nc.tensor.matmul_mx(
-                bank[:], lhsT=w1_w[:, cols].bitcast(FP8X4), lhsT_scale=w1_s[:, cols],
-                rhs=offs_w[:].bitcast(FP8X4), rhs_scale=offs_s[:], start=True, stop=True,
+                bank, lhsT=left_w[:, cols].bitcast(FP8X4), lhsT_scale=left_s[:, cols],
+                rhs=right_w.bitcast(FP8X4), rhs_scale=right_s, start=True, stop=True,
             )
-            y_ps.append(bank)
+
+        y_rows = [keep.tile([P, WINDOW], F32, name=f"y{t}") for t in range(TILES)]
+        for u, part in enumerate(halves):
+            for t in range(FIRST):
+                bank = psum.tile([P, HALF], F32, name=f"y_ps{t}_{u}", tag=f"bank{TILES * u + t}")
+                product(bank[:], t, w1_w, w1_s, offs_w[:, part], offs_s[:, part])
+                nc.scalar.activation(y_rows[t][:, part], bank[:], COPY, scale=gain[:, t : t + 1])
+        y_ps = {}
+        for t in range(FIRST, TILES):
+            y_ps[t] = psum.tile([P, S], F32, name=f"y_ps{t}", tag=f"bank{t}")
+            product(y_ps[t][:], t, w1_w, w1_s, offs_w[:], offs_s[:])
 
         cand_w = gather_words_dealt("cand_w", l_cand)
-        cb_s = deal_scales("cb_s", gather_scales("cb_s_picked", l_cb))
+        cb_s_picked = gather_scales("cb_s_picked", l_cb)
         cb_w = gather_words_dealt("cb_w", l_cb)
+        cand_s = deal_scales("cand_s", cand_s_picked)
+        cb_s = deal_scales("cb_s", cb_s_picked)
 
         wb_b = keep.tile([P, S * PACK], BF16, name="wb_b", align_bytes=64)
         for u in range(2):
             nc.vector.tensor_copy(
-                wb_b[:, u * S * 2 : (u + 1) * S * 2].rearrange("p (c i j) -> p c j i", i=4, j=PACK),
+                wb_b[:, u * HALF * PACK : (u + 1) * HALF * PACK].rearrange("p (c i j) -> p c j i", i=4, j=PACK),
                 wb_raw[u][:].rearrange("p j (c i) -> p c j i", i=4),
             )
         wb_w = keep.tile([P, S], U32, name="wb_w", align_bytes=64)
         wb_s = keep.tile([P, S], U8, name="wb_s", align_bytes=64)
         nc.vector.quantize_mx(wb_w[:].bitcast(FP8X4), wb_s[:], wb_b[:])
 
-        low = keep.tile([P, TILES, S], F32, name="low")
-        upper = keep.tile([P, TILES, S], F32, name="upper")
-        for t in range(TILES):
-            y = keep.tile([P, WINDOW], F32, name=f"y{t}")
-            nc.scalar.activation(y[:, :S], y_ps[t][:], COPY, scale=gain[:, t : t + 1])
-            pa = keep.tile([P, S], F32, name=f"pa{t}")
-            pb = keep.tile([P, S], F32, name=f"pb{t}")
-            high = keep.tile([P, S], F32, name=f"high{t}")
-            nc.scalar.activation(pa[:], y[:].indirect(l_n1[:]), COPY)
-            nc.scalar.activation(pb[:], y[:].indirect(l_n2[:]), COPY)
-            nc.vector.tensor_tensor(low[:, t, :], y[:, :S], pa[:], ALU.min)
-            nc.vector.tensor_tensor(high[:], y[:, :S], pa[:], ALU.max)
-            nc.vector.tensor_tensor(upper[:, t, :], high[:], pb[:], ALU.min)
-
-        z_b = keep.tile([P, S * PACK], BF16, name="z_b", align_bytes=64)
         z_w = keep.tile([P, S], U32, name="z_w", align_bytes=64)
         z_s = keep.tile([P, S], U8, name="z_s", align_bytes=64)
-        half = S // 2
-        for u in range(2):
-            cols = slice(u * half, (u + 1) * half)
-            nc.vector.tensor_tensor(
-                z_b[:, u * half * PACK : (u + 1) * half * PACK].rearrange("p (c i t) -> p c t i", i=4, t=TILES),
-                low[:, :, cols].rearrange("p t (c i) -> p c t i", i=4),
-                upper[:, :, cols].rearrange("p t (c i) -> p c t i", i=4),
-                ALU.max,
-            )
-        for u in range(2):
-            cols = slice(u * half, (u + 1) * half)
-            nc.vector.quantize_mx(
-                z_w[:, cols].bitcast(FP8X4), z_s[:, cols], z_b[:, u * half * PACK : (u + 1) * half * PACK]
-            )
+        early, late = slice(0, EARLY), slice(EARLY, S)
+        early_ps = []
+        for u, part in enumerate((early, late)):
+            width = part.stop - part.start
+            low = keep.tile([P, TILES, width], BF16, name=f"low{u}")
+            upper = keep.tile([P, TILES, width], BF16, name=f"upper{u}", tag=f"upper{u}", align_bytes=64)
+            for t in range(TILES):
+                y = y_rows[t]
+                if u == 0 and t >= FIRST:
+                    nc.scalar.activation(y[:, :S], y_ps[t][:], COPY, scale=gain[:, t : t + 1])
+                pa = keep.tile([P, width], BF16, name=f"pa{t}_{u}")
+                pb = keep.tile([P, width], BF16, name=f"pb{t}_{u}")
+                high = keep.tile([P, width], BF16, name=f"high{t}_{u}")
+                nc.scalar.activation(pa[:], y[:].indirect(entries(l_n1, part)), COPY)
+                if (u, t) in ((0, 2),):
+                    nc.vector.tensor_copy(pb[:], y[:].indirect(entries(l_n2, part)))
+                else:
+                    nc.scalar.activation(pb[:], y[:].indirect(entries(l_n2, part)), COPY)
+                nc.vector.tensor_tensor(high[:], pa[:], pb[:], ALU.max)
+                nc.vector.tensor_tensor(low[:, t, :], pa[:], pb[:], ALU.min)
+                nc.vector.tensor_tensor(upper[:, t, :], high[:], y[:, part], ALU.min)
+            z_b = keep.tile([P, width * PACK], BF16, name=f"z_b{u}", tag=f"z_b{u}", align_bytes=64)
+            pieces = [slice(0, 128), slice(128, 256)]
+            for cols in pieces:
+                nc.vector.tensor_tensor(
+                    z_b[:, cols.start * PACK : cols.stop * PACK].rearrange("p (c i t) -> p c t i", i=4, t=TILES),
+                    low[:, :, cols].rearrange("p t (c i) -> p c t i", i=4),
+                    upper[:, :, cols].rearrange("p t (c i) -> p c t i", i=4),
+                    ALU.max,
+                )
+            for cols in pieces:
+                place = slice(part.start + cols.start, part.start + cols.stop)
+                nc.vector.quantize_mx(
+                    z_w[:, place].bitcast(FP8X4), z_s[:, place], z_b[:, cols.start * PACK : cols.stop * PACK]
+                )
+            if u == 0:
+                for t in range(SPLIT):
+                    bank = psum.tile([P, EARLY], F32, name=f"a_early{t}", tag=f"bank{t}")
+                    for cols in (slice(0, 256),):
+                        product(bank[:, cols], t, cand_w, cand_s, z_w[:, cols], z_s[:, cols])
+                    early_ps.append(bank)
 
-        b_rows = []
-        for t in range(TILES):
-            cols = slice(t * P, (t + 1) * P)
-            bank = psum.tile([P, S], F32, name=f"b_ps{t}", tag=f"bank{TILES + t}")
-            nc.tensor.matmul_mx(
-                bank[:], lhsT=cb_w[:, cols].bitcast(FP8X4), lhsT_scale=cb_s[:, cols],
-                rhs=wb_w[:].bitcast(FP8X4), rhs_scale=wb_s[:], start=True, stop=True,
-            )
-            b = keep.tile([P, WINDOW], F32, name=f"b{t}")
-            nc.scalar.activation(b[:, :S], bank[:], COPY)
-            b_rows.append(b)
+        a_rows = [
+            keep.tile([P, WINDOW], F32, name=f"a{t}", tag=("upper1", "z_b1", "a2", "a3")[t], align_bytes=64)
+            for t in range(TILES)
+        ]
+        late_ps = []
+        for t in range(SPLIT):
+            bank = psum.tile([P, S - EARLY], F32, name=f"a_late{t}", tag=f"bank{2 + t}")
+            product(bank[:], t, cand_w, cand_s, z_w[:, late], z_s[:, late])
+            late_ps.append(bank)
+        for t in range(SPLIT):
+            nc.vector.tensor_scalar(a_rows[t][:, early], early_ps[t][:], 0.0625, None, ALU.mult)
+        for t in range(SPLIT):
+            nc.vector.tensor_scalar(a_rows[t][:, late], late_ps[t][:], 0.0625, None, ALU.mult)
 
         out_rows = out.rearrange("(q t b) j -> t q b j", t=TILES, b=4)
+
+        def finish(t, s1, s2, part):
+            best = keep.tile([P, part.stop - part.start], F32, name=f"best{t}_{part.start}")
+            nc.vector.tensor_tensor(best[:], s1[:, part], s2[:, part], ALU.max)
+            nc.sync.dma_start(out_rows[t][:, :, part], best[:])
+
+        waiting = None
         for t in range(TILES):
-            cols = slice(t * P, (t + 1) * P)
-            a = keep.tile([P, WINDOW], F32, name=f"a{t}")
-            if t == 0:
-                for u in range(2):
-                    part = slice(u * half, (u + 1) * half)
-                    bank = psum.tile([P, half], F32, name=f"a_ps0_{u}", tag=f"bank{TILES * u}")
-                    nc.tensor.matmul_mx(
-                        bank[:], lhsT=cand_w[:, cols].bitcast(FP8X4), lhsT_scale=cand_s[:, cols],
-                        rhs=z_w[:, part].bitcast(FP8X4), rhs_scale=z_s[:, part], start=True, stop=True,
-                    )
-                    nc.vector.tensor_scalar(a[:, part], bank[:], 0.0625, None, ALU.mult)
-            else:
-                bank = psum.tile([P, S], F32, name=f"a_ps{t}", tag=f"bank{t}")
-                nc.tensor.matmul_mx(
-                    bank[:], lhsT=cand_w[:, cols].bitcast(FP8X4), lhsT_scale=cand_s[:, cols],
-                    rhs=z_w[:].bitcast(FP8X4), rhs_scale=z_s[:], start=True, stop=True,
-                )
+            a = a_rows[t]
+            if t >= SPLIT:
+                bank = psum.tile([P, S], F32, name=f"a_ps{t}", tag=f"bank{t - 2}")
+                product(bank[:], t, cand_w, cand_s, z_w[:], z_s[:])
                 nc.scalar.activation(a[:, :S], bank[:], COPY, scale=0.0625)
-            b5 = keep.tile([P, S], F32, name=f"b5_{t}", tag="b5", bufs=2)
-            b6 = keep.tile([P, S], F32, name=f"b6_{t}", tag="b6", bufs=2)
-            nc.scalar.activation(b5[:], b_rows[t][:].indirect(l_n5[:]), COPY)
-            nc.scalar.activation(b6[:], b_rows[t][:].indirect(l_n6[:]), COPY)
+            bank = psum.tile([P, S], F32, name=f"b_ps{t}", tag=f"bank{TILES + t}")
+            product(bank[:], t, cb_w, cb_s, wb_w[:], wb_s[:])
+            b = keep.tile([P, WINDOW], F32, name=f"b{t}")
+            nc.scalar.activation(b[:, :S], bank[:], COPY)
+            b5 = keep.tile([P, S], F32, name=f"b5_{t}", tag="b_picked", bufs=BUFS)
+            nc.scalar.activation(b5[:], b[:].indirect(l_n5[:]), COPY)
+            b6 = keep.tile([P, S], F32, name=f"b6_{t}", tag="b_picked", bufs=BUFS)
             s1 = keep.tile([P, S], F32, name=f"s1_{t}")
             s2 = keep.tile([P, S], F32, name=f"s2_{t}")
+            parts = halves if t == TILES - 1 else [slice(0, S)]
+            for part in parts:
+                nc.scalar.activation(b6[:, part], b[:].indirect(entries(l_n6, part)), COPY)
             nc.vector.tensor_tensor(s1[:], a[:].indirect(l_n3[:]), b5[:], ALU.add)
+            if waiting is not None:
+                finish(*waiting, slice(0, S))
             if t == TILES - 1:
-                a4 = keep.tile([P, S], F32, name="a4")
-                nc.scalar.activation(a4[:], a[:].indirect(l_n4[:]), COPY)
-                nc.vector.tensor_tensor(s2[:], a4[:], b6[:], ALU.add)
-            else:
-                nc.vector.tensor_tensor(s2[:], a[:].indirect(l_n4[:]), b6[:], ALU.add)
-            best = keep.tile([P, S], F32, name=f"best{t}")
-            nc.vector.tensor_tensor(best[:], s1[:], s2[:], ALU.max)
-            nc.sync.dma_start(out_rows[t], best[:])
+                a4 = keep.tile([P, S], F32, name="a4", tag="b_picked", bufs=BUFS)
+            for part in parts:
+                if t == TILES - 1 and part.start in (0, HALF):
+                    nc.scalar.activation(a4[:, part], a[:].indirect(entries(l_n4, part)), COPY)
+                    nc.vector.tensor_tensor(s2[:, part], a4[:, part], b6[:, part], ALU.add)
+                else:
+                    nc.vector.tensor_tensor(s2[:, part], a[:].indirect(entries(l_n4, part)), b6[:, part], ALU.add)
+            waiting = (t, s1, s2)
+        for part in halves:
+            finish(*waiting, part)

@@ -142,9 +142,10 @@ def tile_picked_cdswpathbmed_none_p_kernel(
 
         wb_b = keep.tile([P, S * PACK], BF16, name="wb_b", align_bytes=64)
         for u in range(2):
-            nc.vector.tensor_copy(
-                wb_b[:, u * HALF * PACK : (u + 1) * HALF * PACK].rearrange("p (c i j) -> p c j i", i=4, j=PACK),
-                wb_raw[u][:].rearrange("p j (c i) -> p c j i", i=4),
+            nc.gpsimd.tensor_scalar(
+                wb_b[:, u * HALF * PACK : (u + 1) * HALF * PACK].rearrange("p (n j) -> p n j", j=PACK),
+                wb_raw[u][:].rearrange("p j n -> p n j"),
+                1.0, 0.0, ALU.mult, ALU.add,
             )
         wb_w = keep.tile([P, S], U32, name="wb_w", align_bytes=64)
         wb_s = keep.tile([P, S], U8, name="wb_s", align_bytes=64)
@@ -166,7 +167,7 @@ def tile_picked_cdswpathbmed_none_p_kernel(
                 pb = keep.tile([P, width], BF16, name=f"pb{t}_{u}")
                 high = keep.tile([P, width], BF16, name=f"high{t}_{u}")
                 nc.scalar.activation(pa[:], y[:].indirect(entries(l_n1, part)), COPY)
-                if (u, t) in ((0, 2),):
+                if (u, t) in ((0, 1), (0, 3)):
                     nc.vector.tensor_copy(pb[:], y[:].indirect(entries(l_n2, part)))
                 else:
                     nc.scalar.activation(pb[:], y[:].indirect(entries(l_n2, part)), COPY)

@@ -18,12 +18,13 @@ COPY = mybir.ActivationFunctionType.Copy
 P = 128
 PACK = 4
 TILES = 4
-WINDOW = 2 * S
 HALF = S // 2
-FIRST = 2
-BUFS = 3
-EARLY = 256
-SPLIT = 2
+QUARTER = S // 4
+WINDOW = 2 * S
+Y_BY_HALVES = 2
+A_BY_HALVES = 2
+PICKED_BUFS = 3
+A_SCALE = 0.0625
 
 
 def tile_picked_cdswpathbmed_none_p_kernel(
@@ -34,32 +35,30 @@ def tile_picked_cdswpathbmed_none_p_kernel(
         lists = ctx.enter_context(tc.tile_pool(name="lists", bufs=1))
         keep = ctx.enter_context(tc.tile_pool(name="keep", bufs=1))
         psum = ctx.enter_context(tc.psum_pool(name="psum", bufs=1))
+        halves = [slice(u * HALF, (u + 1) * HALF) for u in range(2)]
 
         def load_list(name, source):
             tile = lists.tile([P, S // 16], U16, name=name)
             nc.sync.dma_start(tile[:], source)
             return tile
 
-        x_s = keep.tile([P, T], U8, name="x_s", align_bytes=64)
-        nc.vector.memset(x_s[:].bitcast(I32), 0)
-
         def load_half(name, weights, u):
             rows = weights.rearrange("(p j) n -> p j n", j=PACK)
             tile = keep.tile([P, PACK, HALF], F32, name=f"{name}{u}")
-            nc.sync.dma_start(tile[:], rows[:, :, u * HALF : (u + 1) * HALF])
+            nc.sync.dma_start(tile[:], rows[:, :, halves[u]])
             return tile
+
+        x_s = keep.tile([P, T], U8, name="x_s", align_bytes=64)
+        nc.vector.memset(x_s[:].bitcast(I32), 0)
 
         l_cand = load_list("l_cand", cand)
         w1_raw = [load_half("w1_raw", w1, 0)]
         l_offs = load_list("l_offs", offs)
-        for q in range(4):
-            nc.sync.dma_start(
-                x_s[32 * q : 32 * q + 4, :].bitcast(I32),
-                x_scales[0, 4 * q : 4 * q + 4, :].bitcast(I32),
-            )
+        for r in range(4):
+            nc.sync.dma_start(x_s[r:P:32, :].bitcast(I32), x_scales[0, r:16:4, :].bitcast(I32))
         w1_raw.append(load_half("w1_raw", w1, 1))
         x_w = keep.tile([P, T], I32, name="x_w", align_bytes=64)
-        nc.sync.dma_start(x_w[:], x_words[0].rearrange("p n t -> p (n t)").bitcast(I32))
+        nc.sync.dma_start(x_w[:], x_words[0].rearrange("p n j -> p (n j)").bitcast(I32))
         l_cb = load_list("l_cb", cb)
         gain = keep.tile([P, TILES], F32, name="gain")
         nc.sync.dma_start(gain[:], gs.rearrange("(p t) o -> p (t o)", t=TILES))
@@ -71,12 +70,12 @@ def tile_picked_cdswpathbmed_none_p_kernel(
         l_n3 = load_list("l_n3", n3)
         l_n4 = load_list("l_n4", n4)
 
-        def entries(tile, part):
-            return tile[:, part.start // 16 : part.stop // 16]
+        def entries(list_tile, part):
+            return list_tile[:, part.start // 16 : part.stop // 16]
 
-        def gather_scales(name, picks):
+        def gather_scales(name, list_tile):
             picked = keep.tile([P, S], U8, name=name, align_bytes=64)
-            nc.vector.tensor_copy(picked[:], x_s[:].indirect(picks[:]))
+            nc.vector.tensor_copy(picked[:], x_s[:].indirect(list_tile[:]))
             return picked
 
         def deal_scales(name, picked):
@@ -87,15 +86,20 @@ def tile_picked_cdswpathbmed_none_p_kernel(
             )
             return dealt
 
-        def gather_words_dealt(name, picks):
+        def gather_words_dealt(name, list_tile):
             dealt = keep.tile([P, S], U32, name=name, align_bytes=64)
             nc.vector.tensor_copy(
-                dealt[:].rearrange("p (t q b) -> p q t b", t=TILES, b=4),
-                x_w[:].bitcast(U32).indirect(picks[:]),
+                dealt[:].rearrange("p (t q e) -> p q t e", t=TILES, e=4),
+                x_w[:].bitcast(U32).indirect(list_tile[:]),
             )
             return dealt
 
-        halves = [slice(u * HALF, (u + 1) * HALF) for u in range(2)]
+        def product(bank, t, left_w, left_s, right_w, right_s):
+            cols = slice(t * P, (t + 1) * P)
+            nc.tensor.matmul_mx(
+                bank, lhsT=left_w[:, cols].bitcast(FP8X4), lhsT_scale=left_s[:, cols],
+                rhs=right_w.bitcast(FP8X4), rhs_scale=right_s, start=True, stop=True,
+            )
 
         cand_s_picked = gather_scales("cand_s_picked", l_cand)
         offs_s = gather_scales("offs_s", l_offs)
@@ -116,21 +120,14 @@ def tile_picked_cdswpathbmed_none_p_kernel(
         for part in halves:
             nc.vector.tensor_copy(offs_w[:, part], x_w[:].bitcast(U32).indirect(entries(l_offs, part)))
 
-        def product(bank, t, left_w, left_s, right_w, right_s):
-            cols = slice(t * P, (t + 1) * P)
-            nc.tensor.matmul_mx(
-                bank, lhsT=left_w[:, cols].bitcast(FP8X4), lhsT_scale=left_s[:, cols],
-                rhs=right_w.bitcast(FP8X4), rhs_scale=right_s, start=True, stop=True,
-            )
-
         y_rows = [keep.tile([P, WINDOW], F32, name=f"y{t}") for t in range(TILES)]
         for u, part in enumerate(halves):
-            for t in range(FIRST):
+            for t in range(Y_BY_HALVES):
                 bank = psum.tile([P, HALF], F32, name=f"y_ps{t}_{u}", tag=f"bank{TILES * u + t}")
                 product(bank[:], t, w1_w, w1_s, offs_w[:, part], offs_s[:, part])
                 nc.scalar.activation(y_rows[t][:, part], bank[:], COPY, scale=gain[:, t : t + 1])
         y_ps = {}
-        for t in range(FIRST, TILES):
+        for t in range(Y_BY_HALVES, TILES):
             y_ps[t] = psum.tile([P, S], F32, name=f"y_ps{t}", tag=f"bank{t}")
             product(y_ps[t][:], t, w1_w, w1_s, offs_w[:], offs_s[:])
 
@@ -141,9 +138,9 @@ def tile_picked_cdswpathbmed_none_p_kernel(
         cb_s = deal_scales("cb_s", cb_s_picked)
 
         wb_b = keep.tile([P, S * PACK], BF16, name="wb_b", align_bytes=64)
-        for u in range(2):
+        for u, part in enumerate(halves):
             nc.gpsimd.tensor_scalar(
-                wb_b[:, u * HALF * PACK : (u + 1) * HALF * PACK].rearrange("p (n j) -> p n j", j=PACK),
+                wb_b[:, part.start * PACK : part.stop * PACK].rearrange("p (n j) -> p n j", j=PACK),
                 wb_raw[u][:].rearrange("p j n -> p n j"),
                 1.0, 0.0, ALU.mult, ALU.add,
             )
@@ -153,99 +150,92 @@ def tile_picked_cdswpathbmed_none_p_kernel(
 
         z_w = keep.tile([P, S], U32, name="z_w", align_bytes=64)
         z_s = keep.tile([P, S], U8, name="z_s", align_bytes=64)
-        early, late = slice(0, EARLY), slice(EARLY, S)
-        early_ps = []
-        for u, part in enumerate((early, late)):
-            width = part.stop - part.start
-            low = keep.tile([P, TILES, width], BF16, name=f"low{u}")
-            upper = keep.tile([P, TILES, width], BF16, name=f"upper{u}", tag=f"upper{u}", align_bytes=64)
+        a_first_ps = []
+        for u, part in enumerate(halves):
+            low = keep.tile([P, TILES, HALF], BF16, name=f"low{u}")
+            upper = keep.tile([P, TILES, HALF], BF16, name=f"upper{u}", tag=f"upper{u}", align_bytes=64)
             for t in range(TILES):
                 y = y_rows[t]
-                if u == 0 and t >= FIRST:
+                if u == 0 and t >= Y_BY_HALVES:
                     nc.scalar.activation(y[:, :S], y_ps[t][:], COPY, scale=gain[:, t : t + 1])
-                pa = keep.tile([P, width], BF16, name=f"pa{t}_{u}")
-                pb = keep.tile([P, width], BF16, name=f"pb{t}_{u}")
-                high = keep.tile([P, width], BF16, name=f"high{t}_{u}")
+                pa = keep.tile([P, HALF], BF16, name=f"pa{t}_{u}")
+                pb = keep.tile([P, HALF], BF16, name=f"pb{t}_{u}")
+                high = keep.tile([P, HALF], BF16, name=f"high{t}_{u}")
                 nc.scalar.activation(pa[:], y[:].indirect(entries(l_n1, part)), COPY)
-                if (u, t) in ((0, 1), (0, 3)):
+                if u == 0 and t % 2 == 1:
                     nc.vector.tensor_copy(pb[:], y[:].indirect(entries(l_n2, part)))
                 else:
                     nc.scalar.activation(pb[:], y[:].indirect(entries(l_n2, part)), COPY)
                 nc.vector.tensor_tensor(high[:], pa[:], pb[:], ALU.max)
                 nc.vector.tensor_tensor(low[:, t, :], pa[:], pb[:], ALU.min)
                 nc.vector.tensor_tensor(upper[:, t, :], high[:], y[:, part], ALU.min)
-            z_b = keep.tile([P, width * PACK], BF16, name=f"z_b{u}", tag=f"z_b{u}", align_bytes=64)
-            pieces = [slice(0, 128), slice(128, 256)]
-            for cols in pieces:
+            z_b = keep.tile([P, HALF * PACK], BF16, name=f"z_b{u}", tag=f"z_b{u}", align_bytes=64)
+            quarters = [slice(v * QUARTER, (v + 1) * QUARTER) for v in range(2)]
+            for cols in quarters:
                 nc.vector.tensor_tensor(
                     z_b[:, cols.start * PACK : cols.stop * PACK].rearrange("p (c i t) -> p c t i", i=4, t=TILES),
                     low[:, :, cols].rearrange("p t (c i) -> p c t i", i=4),
                     upper[:, :, cols].rearrange("p t (c i) -> p c t i", i=4),
                     ALU.max,
                 )
-            for cols in pieces:
+            for cols in quarters:
                 place = slice(part.start + cols.start, part.start + cols.stop)
                 nc.vector.quantize_mx(
                     z_w[:, place].bitcast(FP8X4), z_s[:, place], z_b[:, cols.start * PACK : cols.stop * PACK]
                 )
             if u == 0:
-                for t in range(SPLIT):
-                    bank = psum.tile([P, EARLY], F32, name=f"a_early{t}", tag=f"bank{t}")
-                    for cols in (slice(0, 256),):
-                        product(bank[:, cols], t, cand_w, cand_s, z_w[:, cols], z_s[:, cols])
-                    early_ps.append(bank)
+                for t in range(A_BY_HALVES):
+                    bank = psum.tile([P, HALF], F32, name=f"a_first{t}", tag=f"bank{t}")
+                    product(bank[:], t, cand_w, cand_s, z_w[:, part], z_s[:, part])
+                    a_first_ps.append(bank)
 
-        a_rows = [
-            keep.tile([P, WINDOW], F32, name=f"a{t}", tag=("upper1", "z_b1", "a2", "a3")[t], align_bytes=64)
-            for t in range(TILES)
-        ]
-        late_ps = []
-        for t in range(SPLIT):
-            bank = psum.tile([P, S - EARLY], F32, name=f"a_late{t}", tag=f"bank{2 + t}")
-            product(bank[:], t, cand_w, cand_s, z_w[:, late], z_s[:, late])
-            late_ps.append(bank)
-        for t in range(SPLIT):
-            nc.vector.tensor_scalar(a_rows[t][:, early], early_ps[t][:], 0.0625, None, ALU.mult)
-        for t in range(SPLIT):
-            nc.vector.tensor_scalar(a_rows[t][:, late], late_ps[t][:], 0.0625, None, ALU.mult)
+        a_tags = ["upper1", "z_b1", "a2", "a3"]
+        a_rows = [keep.tile([P, WINDOW], F32, name=f"a{t}", tag=a_tags[t], align_bytes=64) for t in range(TILES)]
+        a_second_ps = []
+        for t in range(A_BY_HALVES):
+            bank = psum.tile([P, HALF], F32, name=f"a_second{t}", tag=f"bank{A_BY_HALVES + t}")
+            product(bank[:], t, cand_w, cand_s, z_w[:, halves[1]], z_s[:, halves[1]])
+            a_second_ps.append(bank)
+        for part, banks in zip(halves, (a_first_ps, a_second_ps)):
+            for t in range(A_BY_HALVES):
+                nc.vector.tensor_scalar(a_rows[t][:, part], banks[t][:], A_SCALE, None, ALU.mult)
 
-        out_rows = out.rearrange("(q t b) j -> t q b j", t=TILES, b=4)
+        out_rows = out.rearrange("(q t e) j -> t q e j", t=TILES, e=4)
 
-        def finish(t, s1, s2, part):
+        def finish(t, sum1, sum2, part):
             best = keep.tile([P, part.stop - part.start], F32, name=f"best{t}_{part.start}")
-            nc.vector.tensor_tensor(best[:], s1[:, part], s2[:, part], ALU.max)
+            nc.vector.tensor_tensor(best[:], sum1[:, part], sum2[:, part], ALU.max)
             nc.sync.dma_start(out_rows[t][:, :, part], best[:])
 
         waiting = None
         for t in range(TILES):
+            last = t == TILES - 1
             a = a_rows[t]
-            if t >= SPLIT:
-                bank = psum.tile([P, S], F32, name=f"a_ps{t}", tag=f"bank{t - 2}")
+            if t >= A_BY_HALVES:
+                bank = psum.tile([P, S], F32, name=f"a_ps{t}", tag=f"bank{t - A_BY_HALVES}")
                 product(bank[:], t, cand_w, cand_s, z_w[:], z_s[:])
-                nc.scalar.activation(a[:, :S], bank[:], COPY, scale=0.0625)
+                nc.scalar.activation(a[:, :S], bank[:], COPY, scale=A_SCALE)
             bank = psum.tile([P, S], F32, name=f"b_ps{t}", tag=f"bank{TILES + t}")
             product(bank[:], t, cb_w, cb_s, wb_w[:], wb_s[:])
             b = keep.tile([P, WINDOW], F32, name=f"b{t}")
             nc.scalar.activation(b[:, :S], bank[:], COPY)
-            b5 = keep.tile([P, S], F32, name=f"b5_{t}", tag="b_picked", bufs=BUFS)
+            b5 = keep.tile([P, S], F32, name=f"b5_{t}", tag="picked", bufs=PICKED_BUFS)
             nc.scalar.activation(b5[:], b[:].indirect(l_n5[:]), COPY)
-            b6 = keep.tile([P, S], F32, name=f"b6_{t}", tag="b_picked", bufs=BUFS)
-            s1 = keep.tile([P, S], F32, name=f"s1_{t}")
-            s2 = keep.tile([P, S], F32, name=f"s2_{t}")
-            parts = halves if t == TILES - 1 else [slice(0, S)]
-            for part in parts:
+            b6 = keep.tile([P, S], F32, name=f"b6_{t}", tag="picked", bufs=PICKED_BUFS)
+            sum1 = keep.tile([P, S], F32, name=f"sum1_{t}")
+            sum2 = keep.tile([P, S], F32, name=f"sum2_{t}")
+            for part in halves if last else [slice(0, S)]:
                 nc.scalar.activation(b6[:, part], b[:].indirect(entries(l_n6, part)), COPY)
-            nc.vector.tensor_tensor(s1[:], a[:].indirect(l_n3[:]), b5[:], ALU.add)
+            nc.vector.tensor_tensor(sum1[:], a[:].indirect(l_n3[:]), b5[:], ALU.add)
             if waiting is not None:
                 finish(*waiting, slice(0, S))
-            if t == TILES - 1:
-                a4 = keep.tile([P, S], F32, name="a4", tag="b_picked", bufs=BUFS)
-            for part in parts:
-                if t == TILES - 1 and part.start in (0, HALF):
+            if last:
+                a4 = keep.tile([P, S], F32, name="a4", tag="picked", bufs=PICKED_BUFS)
+                for part in halves:
                     nc.scalar.activation(a4[:, part], a[:].indirect(entries(l_n4, part)), COPY)
-                    nc.vector.tensor_tensor(s2[:, part], a4[:, part], b6[:, part], ALU.add)
-                else:
-                    nc.vector.tensor_tensor(s2[:, part], a[:].indirect(entries(l_n4, part)), b6[:, part], ALU.add)
-            waiting = (t, s1, s2)
+                    nc.vector.tensor_tensor(sum2[:, part], a4[:, part], b6[:, part], ALU.add)
+            else:
+                nc.vector.tensor_tensor(sum2[:], a[:].indirect(l_n4[:]), b6[:], ALU.add)
+            waiting = (t, sum1, sum2)
         for part in halves:
             finish(*waiting, part)

from contextlib import ExitStack

import concourse.mybir as mybir

K, T, S, H, C = 512, 2048, 512, 512, 512
FLOPS = 2 * K * (H * S + C * S + C * S)

F32 = mybir.dt.float32
BF16 = mybir.dt.bfloat16
I32 = mybir.dt.int32
U32 = mybir.dt.uint32
U16 = mybir.dt.uint16
U8 = mybir.dt.uint8
FP8X4 = mybir.dt.float8_e4m3fn_x4
ALU = mybir.AluOpType
COPY = mybir.ActivationFunctionType.Copy

P = 128
PACK = 4
TILES = 4
HALF = S // 2
QUARTER = S // 4
WINDOW = 2 * S
Y_BY_HALVES = 2
A_BY_HALVES = 2
PICKED_BUFS = 3
A_SCALE = 0.0625


def tile_picked_cdswpathbmed_none_p_kernel(
    tc, x_words, x_scales, w1, gs, wb, offs, n1, n2, cand, cb, n3, n4, n5, n6, out
):
    nc = tc.nc
    with ExitStack() as ctx:
        lists = ctx.enter_context(tc.tile_pool(name="lists", bufs=1))
        keep = ctx.enter_context(tc.tile_pool(name="keep", bufs=1))
        psum = ctx.enter_context(tc.psum_pool(name="psum", bufs=1))
        halves = [slice(u * HALF, (u + 1) * HALF) for u in range(2)]

        def load_list(name, source):
            tile = lists.tile([P, S // 16], U16, name=name)
            nc.sync.dma_start(tile[:], source)
            return tile

        def load_half(name, weights, u):
            rows = weights.rearrange("(p j) n -> p j n", j=PACK)
            tile = keep.tile([P, PACK, HALF], F32, name=f"{name}{u}")
            nc.sync.dma_start(tile[:], rows[:, :, halves[u]])
            return tile

        x_s = keep.tile([P, T], U8, name="x_s", align_bytes=64)
        nc.vector.memset(x_s[:].bitcast(I32), 0)

        l_cand = load_list("l_cand", cand)
        w1_raw = [load_half("w1_raw", w1, 0)]
        l_offs = load_list("l_offs", offs)
        for r in range(4):
            nc.sync.dma_start(x_s[r:P:32, :].bitcast(I32), x_scales[0, r:16:4, :].bitcast(I32))
        w1_raw.append(load_half("w1_raw", w1, 1))
        x_w = keep.tile([P, T], I32, name="x_w", align_bytes=64)
        nc.sync.dma_start(x_w[:], x_words[0].rearrange("p n j -> p (n j)").bitcast(I32))
        l_cb = load_list("l_cb", cb)
        gain = keep.tile([P, TILES], F32, name="gain")
        nc.sync.dma_start(gain[:], gs.rearrange("(p t) o -> p (t o)", t=TILES))
        l_n1 = load_list("l_n1", n1)
        l_n2 = load_list("l_n2", n2)
        wb_raw = [load_half("wb_raw", wb, u) for u in range(2)]
        l_n5 = load_list("l_n5", n5)
        l_n6 = load_list("l_n6", n6)
        l_n3 = load_list("l_n3", n3)
        l_n4 = load_list("l_n4", n4)

        def entries(list_tile, part):
            return list_tile[:, part.start // 16 : part.stop // 16]

        def gather_scales(name, list_tile):
            picked = keep.tile([P, S], U8, name=name, align_bytes=64)
            nc.vector.tensor_copy(picked[:], x_s[:].indirect(list_tile[:]))
            return picked

        def deal_scales(name, picked):
            dealt = keep.tile([P, S], U8, name=name, align_bytes=64)
            nc.vector.tensor_copy(
                dealt[:].bitcast(I32).rearrange("p (t q) -> p t q", t=TILES),
                picked[:].bitcast(I32).rearrange("p (q t) -> p t q", t=TILES),
            )
            return dealt

        def gather_words_dealt(name, list_tile):
            dealt = keep.tile([P, S], U32, name=name, align_bytes=64)
            nc.vector.tensor_copy(
                dealt[:].rearrange("p (t q e) -> p q t e", t=TILES, e=4),
                x_w[:].bitcast(U32).indirect(list_tile[:]),
            )
            return dealt

        def product(bank, t, left_w, left_s, right_w, right_s):
            cols = slice(t * P, (t + 1) * P)
            nc.tensor.matmul_mx(
                bank, lhsT=left_w[:, cols].bitcast(FP8X4), lhsT_scale=left_s[:, cols],
                rhs=right_w.bitcast(FP8X4), rhs_scale=right_s, start=True, stop=True,
            )

        cand_s_picked = gather_scales("cand_s_picked", l_cand)
        offs_s = gather_scales("offs_s", l_offs)

        w1_b = keep.tile([P, H * PACK], BF16, name="w1_b", align_bytes=64)
        w1_dealt = w1_b[:].rearrange("p (t m j) -> p m j t", t=TILES, j=PACK)
        for u in range(2):
            nc.scalar.activation(
                w1_dealt[:, u * (P // 2) : (u + 1) * (P // 2)],
                w1_raw[u][:].rearrange("p j (m t) -> p m j t", t=TILES),
                COPY,
            )
        w1_w = keep.tile([P, H], U32, name="w1_w", align_bytes=64)
        w1_s = keep.tile([P, H], U8, name="w1_s", align_bytes=64)
        nc.vector.quantize_mx(w1_w[:].bitcast(FP8X4), w1_s[:], w1_b[:])

        offs_w = keep.tile([P, S], U32, name="offs_w", align_bytes=64)
        for part in halves:
            nc.vector.tensor_copy(offs_w[:, part], x_w[:].bitcast(U32).indirect(entries(l_offs, part)))

        y_rows = [keep.tile([P, WINDOW], F32, name=f"y{t}") for t in range(TILES)]
        for u, part in enumerate(halves):
            for t in range(Y_BY_HALVES):
                bank = psum.tile([P, HALF], F32, name=f"y_ps{t}_{u}", tag=f"bank{TILES * u + t}")
                product(bank[:], t, w1_w, w1_s, offs_w[:, part], offs_s[:, part])
                nc.scalar.activation(y_rows[t][:, part], bank[:], COPY, scale=gain[:, t : t + 1])
        y_ps = {}
        for t in range(Y_BY_HALVES, TILES):
            y_ps[t] = psum.tile([P, S], F32, name=f"y_ps{t}", tag=f"bank{t}")
            product(y_ps[t][:], t, w1_w, w1_s, offs_w[:], offs_s[:])

        cand_w = gather_words_dealt("cand_w", l_cand)
        cb_s_picked = gather_scales("cb_s_picked", l_cb)
        cb_w = gather_words_dealt("cb_w", l_cb)
        cand_s = deal_scales("cand_s", cand_s_picked)
        cb_s = deal_scales("cb_s", cb_s_picked)

        wb_b = keep.tile([P, S * PACK], BF16, name="wb_b", align_bytes=64)
        for u, part in enumerate(halves):
            nc.gpsimd.tensor_scalar(
                wb_b[:, part.start * PACK : part.stop * PACK].rearrange("p (n j) -> p n j", j=PACK),
                wb_raw[u][:].rearrange("p j n -> p n j"),
                1.0, 0.0, ALU.mult, ALU.add,
            )
        wb_w = keep.tile([P, S], U32, name="wb_w", align_bytes=64)
        wb_s = keep.tile([P, S], U8, name="wb_s", align_bytes=64)
        nc.vector.quantize_mx(wb_w[:].bitcast(FP8X4), wb_s[:], wb_b[:])

        z_w = keep.tile([P, S], U32, name="z_w", align_bytes=64)
        z_s = keep.tile([P, S], U8, name="z_s", align_bytes=64)
        a_first_ps = []
        for u, part in enumerate(halves):
            low = keep.tile([P, TILES, HALF], BF16, name=f"low{u}")
            upper = keep.tile([P, TILES, HALF], BF16, name=f"upper{u}", tag=f"upper{u}", align_bytes=64)
            for t in range(TILES):
                y = y_rows[t]
                if u == 0 and t >= Y_BY_HALVES:
                    nc.scalar.activation(y[:, :S], y_ps[t][:], COPY, scale=gain[:, t : t + 1])
                pa = keep.tile([P, HALF], BF16, name=f"pa{t}_{u}")
                pb = keep.tile([P, HALF], BF16, name=f"pb{t}_{u}")
                high = keep.tile([P, HALF], BF16, name=f"high{t}_{u}")
                nc.scalar.activation(pa[:], y[:].indirect(entries(l_n1, part)), COPY)
                if u == 0 and t % 2 == 1:
                    nc.vector.tensor_copy(pb[:], y[:].indirect(entries(l_n2, part)))
                else:
                    nc.scalar.activation(pb[:], y[:].indirect(entries(l_n2, part)), COPY)
                nc.vector.tensor_tensor(high[:], pa[:], pb[:], ALU.max)
                nc.vector.tensor_tensor(low[:, t, :], pa[:], pb[:], ALU.min)
                nc.vector.tensor_tensor(upper[:, t, :], high[:], y[:, part], ALU.min)
            z_b = keep.tile([P, HALF * PACK], BF16, name=f"z_b{u}", tag=f"z_b{u}", align_bytes=64)
            quarters = [slice(v * QUARTER, (v + 1) * QUARTER) for v in range(2)]
            for cols in quarters:
                nc.vector.tensor_tensor(
                    z_b[:, cols.start * PACK : cols.stop * PACK].rearrange("p (c i t) -> p c t i", i=4, t=TILES),
                    low[:, :, cols].rearrange("p t (c i) -> p c t i", i=4),
                    upper[:, :, cols].rearrange("p t (c i) -> p c t i", i=4),
                    ALU.max,
                )
            for cols in quarters:
                place = slice(part.start + cols.start, part.start + cols.stop)
                nc.vector.quantize_mx(
                    z_w[:, place].bitcast(FP8X4), z_s[:, place], z_b[:, cols.start * PACK : cols.stop * PACK]
                )
            if u == 0:
                for t in range(A_BY_HALVES):
                    bank = psum.tile([P, HALF], F32, name=f"a_first{t}", tag=f"bank{t}")
                    product(bank[:], t, cand_w, cand_s, z_w[:, part], z_s[:, part])
                    a_first_ps.append(bank)

        a_tags = ["upper1", "z_b1", "a2", "a3"]
        a_rows = [keep.tile([P, WINDOW], F32, name=f"a{t}", tag=a_tags[t], align_bytes=64) for t in range(TILES)]
        a_second_ps = []
        for t in range(A_BY_HALVES):
            bank = psum.tile([P, HALF], F32, name=f"a_second{t}", tag=f"bank{A_BY_HALVES + t}")
            product(bank[:], t, cand_w, cand_s, z_w[:, halves[1]], z_s[:, halves[1]])
            a_second_ps.append(bank)
        for part, banks in zip(halves, (a_first_ps, a_second_ps)):
            for t in range(A_BY_HALVES):
                nc.vector.tensor_scalar(a_rows[t][:, part], banks[t][:], A_SCALE, None, ALU.mult)

        out_rows = out.rearrange("(q t e) j -> t q e j", t=TILES, e=4)

        def finish(t, sum1, sum2, part):
            best = keep.tile([P, part.stop - part.start], F32, name=f"best{t}_{part.start}")
            nc.vector.tensor_tensor(best[:], sum1[:, part], sum2[:, part], ALU.max)
            nc.sync.dma_start(out_rows[t][:, :, part], best[:])

        waiting = None
        for t in range(TILES):
            last = t == TILES - 1
            a = a_rows[t]
            if t >= A_BY_HALVES:
                bank = psum.tile([P, S], F32, name=f"a_ps{t}", tag=f"bank{t - A_BY_HALVES}")
                product(bank[:], t, cand_w, cand_s, z_w[:], z_s[:])
                nc.scalar.activation(a[:, :S], bank[:], COPY, scale=A_SCALE)
            bank = psum.tile([P, S], F32, name=f"b_ps{t}", tag=f"bank{TILES + t}")
            product(bank[:], t, cb_w, cb_s, wb_w[:], wb_s[:])
            b = keep.tile([P, WINDOW], F32, name=f"b{t}")
            nc.scalar.activation(b[:, :S], bank[:], COPY)
            b5 = keep.tile([P, S], F32, name=f"b5_{t}", tag="picked", bufs=PICKED_BUFS)
            nc.scalar.activation(b5[:], b[:].indirect(l_n5[:]), COPY)
            b6 = keep.tile([P, S], F32, name=f"b6_{t}", tag="picked", bufs=PICKED_BUFS)
            sum1 = keep.tile([P, S], F32, name=f"sum1_{t}")
            sum2 = keep.tile([P, S], F32, name=f"sum2_{t}")
            for part in halves if last else [slice(0, S)]:
                nc.scalar.activation(b6[:, part], b[:].indirect(entries(l_n6, part)), COPY)
            nc.vector.tensor_tensor(sum1[:], a[:].indirect(l_n3[:]), b5[:], ALU.add)
            if waiting is not None:
                finish(*waiting, slice(0, S))
            if last:
                a4 = keep.tile([P, S], F32, name="a4", tag="picked", bufs=PICKED_BUFS)
                for part in halves:
                    nc.scalar.activation(a4[:, part], a[:].indirect(entries(l_n4, part)), COPY)
                    nc.vector.tensor_tensor(sum2[:, part], a4[:, part], b6[:, part], ALU.add)
            else:
                nc.vector.tensor_tensor(sum2[:], a[:].indirect(l_n4[:]), b6[:], ALU.add)
            waiting = (t, sum1, sum2)
        for part in halves:
            finish(*waiting, part)
